import numpy as np, ml_dtypes
CORES = [83,85,87,115,117,119]
N = 6
GR, GC = 3, 2
L, KA, KB, F = 6, 3, 2, 128
def setup_inputs(rng):
    return {"a": rng.standard_normal((N, 128, KA * 128), dtype=np.float32).astype(ml_dtypes.bfloat16), "b": rng.standard_normal((N, 128, KB * F), dtype=np.float32).astype(ml_dtypes.bfloat16)}
def setup_inputs_big(rng):
    d = setup_inputs(rng)
    for k in ("a", "b"): d[k] = (d[k].astype(np.float32) * 1024.0).astype(d[k].dtype)
    return d
def setup_inputs_small(rng):
    d = setup_inputs(rng)
    for k in ("a", "b"): d[k] = (d[k].astype(np.float32) * (1 / 1024.0)).astype(d[k].dtype)
    return d
def setup_inputs_apart(rng):
    d = setup_inputs(rng)
    f = (10.0 ** rng.permutation(np.linspace(-1.5, 1.5, N))).astype(np.float32).reshape(N, 1, 1)
    for k in ("a", "b"): d[k] = (d[k].astype(np.float32) * f).astype(d[k].dtype)
    return d
def reference(a, b):
    A, B = a.astype(np.float64), b.astype(np.float64)
    y = np.zeros((N, 128, F))
    for i in range(GR):
        for j in range(GC):
            for k in range(L):
                At = A[i * GC + k // KA][:, 128 * (k % KA):128 * (k % KA) + 128]
                Bt = B[(k // KB) * GC + j][:, F * (k % KB):F * (k % KB) + F]
                y[i * GC + j] += At.T @ Bt
    return {"y": y.astype(ml_dtypes.bfloat16 if a.dtype != np.float64 else np.float64)}

from concourse.bass import DstId, RemoteDMATransfer

GR, GC = 3, 2
L, KA, KB, F = 6, 3, 2, 128

SCRATCH = {
    "A": ("sbuf", [128, L * 128], "bfloat16"),
    "B": ("sbuf", [128, L * F], "bfloat16"),
    "acc": ("psum", [128, F], "float32"),
    "ysb": ("sbuf", [128, F], "bfloat16"),
}
SEMAPHORES = ["la", "lb", "ra", "rb0", "rb1", "rb2", "sent", "mm", "cp", "st"]


def _engines(m):
    return [e for e in range(m.bit_length()) if (m >> e) & 1]


def _mask(es):
    m = 0
    for e in es:
        m |= 1 << e
    return m


def _plan(rank, cores, topo):
    core = cores[rank]
    row, col = divmod(rank, GC)
    partner = cores[row * GC + (1 - col)]
    peers = [cores[r * GC + col] for r in range(GR) if r != row]

    def away(d):
        return topo.chip(d) != topo.chip(core)

    every, some = ~0, 0
    for d in [partner] + peers:
        every &= topo.mask(core, d)
        some |= topo.mask(core, d)
    far = _engines(every)
    near = _engines(some & ~every) or far

    call_a = [("A", [partner], far if away(partner) else near)]
    call_b = []
    for ds, es in (([d for d in peers if away(d)], far), ([d for d in peers if not away(d)], near)):
        if ds:
            call_b.append(("B", ds, es))
    return [call_a, call_b] if away(partner) else [call_b, call_a]


def rank_program(g, core, T, topo):
    rank = T.rank_of(core)
    if rank is None:
        return
    cores = T.cores
    row, col = divmod(rank, GC)
    sem = T.sem
    own = {"A": T.A[:, KA * col * 128:(KA * col + KA) * 128], "B": T.B[:, KB * row * F:(KB * row + KB) * F]}
    loaded = {"A": sem.la, "B": sem.lb}
    lands = {"A": sem.ra, "B": sem["rb%d" % row]}

    g.sync.dma_start(own["A"], T.a[:, :]).then_inc(sem.la, 16)
    g.scalar.dma_start(own["B"], T.b[:, :]).then_inc(sem.lb, 16)

    sent = 0
    for call in _plan(rank, cores, topo):
        g.wait_ge(loaded[call[0][0]], 16)
        trs = []
        for kind, ds, es in call:
            trs.append(RemoteDMATransfer(
                dst_ids=[DstId(rid=topo.addr(d)[0], pnc=topo.addr(d)[1]) for d in ds],
                dma_engine_mask=_mask(es), remote_sem=lands[kind],
                srcs=[own[kind]], dsts=[own[kind]] * len(ds)))
            sent += len(es)
        g.remote_dma_fused(trs, local_sem=sem.sent)

    src_a, src_b = {col: (0.0, "la", 16)}, {row: (0.0, "lb", 16)}
    for s in range(GR * GC):
        for n, call in enumerate(_plan(s, cores, topo)):
            for kind, ds, es in call:
                if core in ds:
                    when = 1.0 + n + (2.0 if topo.chip(cores[s]) != topo.chip(core) else 0.0)
                    if kind == "A":
                        src_a[s % GC] = (when, "ra", len(es))
                    else:
                        src_b[s // GC] = (when, "rb%d" % (s // GC), len(es))

    order = sorted(range(L), key=lambda k: (max(src_a[k // KA][0], src_b[k // KB][0]), k))
    waited = []
    mm = None
    for n, k in enumerate(order):
        for when, name, count in sorted((src_a[k // KA], src_b[k // KB])):
            if name not in waited:
                g.tensor.wait_ge(sem[name], count)
                waited.append(name)
        mm = g.tensor.matmul(T.acc[:, :], T.A[:, k * 128:(k + 1) * 128], T.B[:, k * F:(k + 1) * F],
                             start=(n == 0), stop=(n == L - 1))
    mm.then_inc(sem.mm, 1)

    g.vector.wait_ge(sem.mm, 1)
    g.vector.tensor_copy(T.ysb[:, :], T.acc[:, :]).then_inc(sem.cp, 1)
    g.sync.wait_ge(sem.cp, 1)
    g.sync.dma_start(T.y[:, :], T.ysb[:, :]).then_inc(sem.st, 16)
    g.sync.wait_ge(sem.st, 16)
    g.wait_ge(sem.sent, sent)
